import numpy as np
import ml_dtypes


def mxq(x, axis, fmt="e4m3"):
    dtype, down = {"e4m3": (ml_dtypes.float8_e4m3fn, 7), "e5m2": (ml_dtypes.float8_e5m2, 14)}[fmt]
    v = np.moveaxis(np.asarray(x, np.float32).astype(ml_dtypes.bfloat16).astype(np.float64), axis, -1)
    blocks = v.reshape(v.shape[:-1] + (-1, 32))
    amax = np.abs(blocks).max(-1, keepdims=True)
    byte = np.maximum(np.where(amax > 0, np.frexp(amax)[1] - 1 + 127, 0) - down, 1)
    scale = np.exp2(byte - 127.0)
    codes = (blocks / scale).astype(np.float32).astype(dtype).astype(np.float64)
    return np.moveaxis((codes * scale).reshape(v.shape), -1, axis)


WIDE = False


def mx_kscale(k):
    if not WIDE:
        return np.ones(k)
    levels = np.array([10, -10, 5, -5, 0])
    if k % 512:
        return np.exp2(np.random.permutation(np.resize(levels, k // 32))).repeat(32)
    a = np.empty((k // 512, 16))
    for p in range(k // 512):
        a[p, :8] = np.random.permutation(np.resize(levels, 8))
        for g in range(8):
            far = levels[np.abs(levels - a[p, g]) >= 10]
            a[p, g + 8] = far[np.random.randint(len(far))]
    return np.exp2(a.ravel()).repeat(32)


BF16 = ml_dtypes.bfloat16


def bf(x):
    return np.asarray(x, np.float32).astype(BF16)


def f64(x):
    return np.asarray(x).astype(np.float64)

def planes(Y):
    n, m = Y.shape
    b = f64(bf(Y)).reshape(n // 32, 32, m)
    amax = np.abs(b).max(1)
    byte = np.clip(np.where(amax > 0, np.frexp(amax)[1] - 1 + 127 - 7, 1), 1, 254)
    codes = (b * np.exp2(127.0 - byte)[:, None, :]).reshape(n, m).astype(np.float32).astype(ml_dtypes.float8_e4m3fn).view(np.uint8)
    words = codes.reshape(n // 512, 128, 4, m).transpose(0, 1, 3, 2)
    return np.ascontiguousarray(words), np.ascontiguousarray(byte.astype(np.uint8).reshape(n // 512, 16, m))


N, M, D, E = 2048, 1024, 512, 512
RADIUS = 16.0
BETA = 2.0


def softmax(a):
    e = np.exp(a - a.max(-1, keepdims=True))
    return e / e.sum(-1, keepdims=True)


def value_time(v, g):
    gv = g[:, None] * v
    return np.sqrt(RADIUS**2 + np.sum(gv * gv, axis=-1))


def setup_inputs():
    s, t = mx_kscale(D), mx_kscale(M)
    c = 0.95 / D**0.25
    return {"q": bf(np.random.standard_normal((N, D)) * c * s),
            "qt": bf(4.6 + 0.15 * np.random.standard_normal(N)),
            "k": bf(np.random.standard_normal((M, D)) * c / s),
            "kt": bf(4.6 + 0.15 * np.random.standard_normal(M)),
            "v": bf(np.random.standard_normal((M, E)) / t[:, None]),
            "g": bf(np.random.standard_normal(M) * t)}


def core(q, qt, k, kt, v, g):
    qt, kt, v, g = f64(qt), f64(kt), f64(v), f64(g)
    l = (mxq(f64(q), 1, "e4m3") @ mxq(f64(k), 1, "e4m3").T) - qt[:, None] * kt[None, :]
    p = softmax(BETA * l)
    pg = p * g[None, :]
    us = mxq(pg, 1, "e4m3") @ mxq(v, 0, "e4m3")
    vt = value_time(v, g)
    ut = np.sum(p * vt[None, :], axis=-1)
    root = np.sqrt(ut * ut - np.sum(us * us, axis=-1))
    return RADIUS * us / root[:, None]


def reference(q, qt, k, kt, v, g):
    R_out = core(q, qt, k, kt, v, g)
    words, scales = planes(R_out)
    return R_out, words, scales

@@ -1,0 +1,408 @@
+from contextlib import ExitStack
+
+import concourse.mybir as mybir
+from concourse.masks import make_identity
+
+N, M, D, E = 2048, 1024, 512, 512
+FLOPS = 2 * N * M * D + 2 * N * M * E
+
+F32 = mybir.dt.float32
+BF16 = mybir.dt.bfloat16
+I32 = mybir.dt.int32
+U32 = mybir.dt.uint32
+U8 = mybir.dt.uint8
+FP8X4 = mybir.dt.float8_e4m3fn_x4
+ALU = mybir.AluOpType
+ACT = mybir.ActivationFunctionType
+
+P = 128
+PACK = 4
+BANK = 512
+TILES = N // P
+RADIUS = 16.0
+BETA = 2.0
+
+
+def tile_lorentzcentroidaggregation_x1_kernel(tc, q, qt, k, kt, v, g, out_0, out_1, out_2):
+    nc = tc.nc
+    with ExitStack() as ctx:
+        keep = ctx.enter_context(tc.tile_pool(name="keep", bufs=1))
+        work = ctx.enter_context(tc.tile_pool(name="work", bufs=2))
+        stat = ctx.enter_context(tc.tile_pool(name="stat", bufs=4))
+        psum = ctx.enter_context(tc.psum_pool(name="psum", bufs=1))
+        ctx.enter_context(tc.manual_schedule())
+
+        def bank(tag):
+            return psum.tile([P, BANK], F32, name=tag, tag=tag)
+
+        def flat(ap3):
+            return ap3.rearrange("p a b -> p (a b)")
+
+        kt_sb = keep.tile([P, 2, PACK], BF16, name="kt_sb")
+        qt_sb = keep.tile([P, 4, PACK], BF16, name="qt_sb")
+        g_sb = keep.tile([P, 2, PACK], BF16, name="g_sb")
+        nc.scalar.dma_start(out=kt_sb[:], in_=kt.rearrange("(h p t) -> p h t", p=P, t=PACK))
+        nc.scalar.dma_start(out=qt_sb[:], in_=qt.rearrange("(h p t) -> p h t", p=P, t=PACK))
+        nc.scalar.dma_start(out=g_sb[:], in_=g.rearrange("(h p t) -> p h t", p=P, t=PACK))
+
+        def rows(src, h):
+            return src[BANK * h : BANK * (h + 1), :].rearrange("(p t) d -> p t d", t=PACK)
+
+        k_sb = [keep.tile([P, PACK, D], BF16, name="k_sb%d" % h) for h in range(2)]
+        v_sb = [keep.tile([P, PACK, E], BF16, name="v_sb%d" % h) for h in range(2)]
+        q_sb = [keep.tile([P, 2, D], BF16, name="q_sb%d" % j) for j in range(TILES // 2)]
+
+        def load_q(j):
+            nc.sync.dma_start(out=q_sb[j][:], in_=rows(q, j // 2)[:, 2 * (j % 2) : 2 * (j % 2) + 2, :])
+
+        nc.sync.dma_start(out=k_sb[0][:], in_=rows(k, 0))
+        load_q(0)
+        nc.sync.dma_start(out=k_sb[1][:], in_=rows(k, 1))
+        nc.sync.dma_start(out=v_sb[0][:], in_=rows(v, 0))
+        nc.sync.dma_start(out=v_sb[1][:], in_=rows(v, 1))
+        for j in range(1, TILES // 2):
+            load_q(j)
+
+        ident = keep.tile([P, P], F32, name="ident")
+        make_identity(nc, ident[:])
+        minus_half = keep.tile([P, PACK], F32, name="minus_half")
+        nc.gpsimd.memset(minus_half[:], -0.5)
+        warm = keep.tile([P, 1], F32, name="warm")
+        nc.scalar.activation(out=warm[:], in_=minus_half[:, 0:1], func=ACT.Exp)
+        kt_f = keep.tile([P, 2 * PACK], F32, name="kt_f")
+        nc.gpsimd.tensor_copy(out=kt_f[:], in_=flat(kt_sb[:]))
+        g16 = keep.tile([P, 2 * PACK], F32, name="g16")
+        nc.gpsimd.tensor_scalar(out=g16[:], in0=flat(g_sb[:]), scalar1=1.0 / RADIUS, scalar2=1.0,
+                                op0=ALU.mult, op1=ALU.mult)
+
+        def spread(col4, tag):
+            b = bank(tag)
+            for t in range(PACK):
+                nc.tensor.transpose(b[:, P * t : P * (t + 1)], col4[:, t : t + 1].to_broadcast([P, P]), ident[:])
+            return b
+
+        def turn_pair(src, tag):
+            b = bank(tag)
+            for s in range(2):
+                words = src[:, s, :].bitcast(F32)
+                for u in range(2):
+                    c = P * (2 * s + u)
+                    nc.tensor.transpose(b[:, c : c + P], words[:, u : D // 2 : 2], ident[:])
+            return b
+
+        def pair_out(on_vector, dst, b):
+            src = b[:].rearrange("p (s u n) -> p s n u", s=2, u=2)
+            dstw = dst.bitcast(F32).rearrange("p (s n u) -> p s n u", s=2, u=2)
+            if on_vector:
+                nc.vector.tensor_copy(out=dstw, in_=src)
+            else:
+                nc.scalar.copy(out=dstw, in_=src)
+
+        def quantize(pool, name, src, bufs):
+            width = src.shape[1] // PACK
+            codes = pool.tile([P, width], U32, name=name + "_c", tag=name + "_c", bufs=bufs, align_bytes=64)
+            scales = pool.tile([P, width], U8, name=name + "_s", tag=name + "_s", bufs=bufs, align_bytes=64)
+            nc.vector.quantize_mx(out=codes[:].bitcast(FP8X4), scales=scales[:], in_=src)
+            return codes, scales
+
+        kt_row = keep.tile([P, M], F32, name="kt_row")
+        vs_row = keep.tile([P, M], F32, name="vs_row")
+        gv = keep.tile([P, 2 * PACK], F32, name="gv")
+        k_il = [keep.tile([P, PACK * BANK], BF16, name="k_il%d" % h, align_bytes=64) for h in range(2)]
+        v_il = [keep.tile([P, E, PACK], BF16, name="v_il%d" % h, align_bytes=64) for h in range(2)]
+        junk = keep.tile([P, BANK], BF16, name="junk")
+
+        k_q, v_q, q_q, q_bank, q_il = {}, {}, {}, {}, {}
+        s_bank, x, bias, e, z, rz, w, ut, t_bank = {}, {}, {}, {}, {}, {}, {}, {}, {}
+        pg_rows, pg_il, pg_q, u_bank, ss, rs = {}, {}, {}, {}, {}, {}
+        res, res_il = {}, {}
+
+        def q_turn(j, tag):
+            q_bank[j] = turn_pair(q_sb[j], tag)
+
+        def q_out(j, on_vector):
+            q_il[j] = work.tile([P, 2 * PACK * P], BF16, name="q_il", tag="q_il", align_bytes=64)
+            pair_out(on_vector, q_il[j][:], q_bank[j])
+
+        def q_quant(j):
+            q_q[j] = quantize(work, "q", q_il[j][:], 3)
+
+        def scores(i, h):
+            codes, scales = q_q[i // 2]
+            c = slice(P * (i % 2), P * (i % 2 + 1))
+            s_bank[i, h] = bank("S%d" % h)
+            nc.tensor.matmul_mx(out=s_bank[i, h][:], lhsT=codes[:, c].bitcast(FP8X4), lhsT_scale=scales[:, c],
+                                rhs=k_q[h][0][:].bitcast(FP8X4), rhs_scale=k_q[h][1][:], start=True, stop=True)
+
+        def logits(i, h):
+            if h == 0:
+                x[i] = work.tile([P, M], F32, name="x", tag="x", bufs=3)
+            c = slice(BANK * h, BANK * (h + 1))
+            nc.vector.scalar_tensor_tensor(out=x[i][:, c], in0=kt_row[:, c], scalar=flat(qt_sb[:])[:, i : i + 1],
+                                           in1=s_bank[i, h][:], op0=ALU.mult, op1=ALU.subtract)
+
+        def row_max(i):
+            bias[i] = stat.tile([P, 1], F32, name="bias", tag="bias")
+            nc.vector.tensor_scalar(out=x[i][:], in0=x[i][:], scalar1=BETA, scalar2=None,
+                                    op0=ALU.mult, op1=ALU.min, accum_out=bias[i][:])
+
+        def exponent(i):
+            e[i] = work.tile([P, M], F32, name="e", tag="e", bufs=3)
+            z[i] = stat.tile([P, 1], F32, name="z", tag="z")
+            nc.scalar.activation(out=e[i][:], in_=x[i][:], func=ACT.Exp, scale=-1.0, bias=bias[i][:],
+                                 accum_out=z[i][:])
+
+        def recip(i):
+            rz[i] = stat.tile([P, 1], F32, name="rz", tag="rz")
+            nc.vector.reciprocal(out=rz[i][:], in_=z[i][:])
+
+        def weigh(i):
+            w[i] = work.tile([P, M], F32, name="w", tag="w")
+            ut[i] = stat.tile([P, 1], F32, name="ut", tag="ut", bufs=8)
+            nc.vector.scalar_tensor_tensor(out=w[i][:], in0=e[i][:], scalar=rz[i][:], in1=vs_row[:],
+                                           op0=ALU.mult, op1=ALU.mult, accum_out=ut[i][:])
+
+        def turn(i, tags=("T0", "T1")):
+            for h in range(2):
+                t_bank[i, h] = bank(tags[h])
+                for t in range(PACK):
+                    c = BANK * h + P * t
+                    nc.tensor.transpose(t_bank[i, h][:, P * t : P * (t + 1)], w[i][:, c : c + P], ident[:])
+
+        def gain_rows(i):
+            pg_rows[i] = work.tile([P, 2, PACK, P], BF16, name="pg_rows", tag="pg_rows", bufs=3)
+            for h in range(2):
+                for t in range(PACK):
+                    j = PACK * h + t
+                    nc.scalar.activation(out=pg_rows[i][:, h, t, :], in_=t_bank[i, h][:, P * t : P * (t + 1)],
+                                         func=ACT.Copy, scale=gv[:, j : j + 1])
+
+        def gpsimd_move(dst, src):
+            nc.gpsimd.tensor_scalar(out=dst, in0=src, scalar1=1.0, scalar2=1.0, op0=ALU.mult, op1=ALU.mult)
+
+        def interleave(i, h):
+            if h == 0:
+                pg_il[i] = work.tile([P, 2, P, PACK], BF16, name="pg_il", tag="pg_il", bufs=1, align_bytes=64)
+            gpsimd_move(pg_il[i][:, h, :, :], pg_rows[i][:, h, :, :].rearrange("p t n -> p n t"))
+
+        def gain_direct(i, h):
+            if h == 0:
+                pg_il[i] = work.tile([P, 2, P, PACK], BF16, name="pg_dir", tag="pg_dir", bufs=2, align_bytes=64)
+            nc.vector.tensor_tensor(
+                out=pg_il[i][:, h, :, :], in0=t_bank[i, h][:].rearrange("p (t n) -> p n t", t=PACK),
+                in1=gv[:, PACK * h : PACK * (h + 1)].unsqueeze(1).to_broadcast([P, P, PACK]), op=ALU.mult)
+
+        def pg_quant(i):
+            pg_q[i] = quantize(work, "pg", pg_il[i][:].rearrange("p h n t -> p (h n t)"), 3)
+
+        def values(i, tag):
+            codes, scales = pg_q[i]
+            u_bank[i] = bank(tag)
+            for h in range(2):
+                c = slice(P * h, P * (h + 1))
+                nc.tensor.matmul_mx(out=u_bank[i][:], lhsT=codes[:, c].bitcast(FP8X4), lhsT_scale=scales[:, c],
+                                    rhs=v_q[h][0][:].bitcast(FP8X4), rhs_scale=v_q[h][1][:],
+                                    start=(h == 0), stop=(h == 1))
+
+        def square_sum(i):
+            ss[i] = stat.tile([P, 1], F32, name="ss", tag="ss")
+            nc.scalar.activation(out=junk[:], in_=u_bank[i][:], func=ACT.Square, scale=1.0 / RADIUS,
+                                 accum_out=ss[i][:])
+
+        def root(i):
+            gap = stat.tile([P, 1], F32, name="gap", tag="gap")
+            rs[i] = stat.tile([P, 1], F32, name="rs", tag="rs")
+            nc.gpsimd.tensor_scalar(out=gap[:], in0=ut[i][:], scalar1=ut[i][:], scalar2=ss[i][:],
+                                    op0=ALU.mult, op1=ALU.subtract)
+            nc.gpsimd.tensor_tensor(out=rs[i][:], in0=gap[:], in1=minus_half[:, 0:1], op=ALU.pow)
+
+        def finish(i, on_vector):
+            grp, t = divmod(i, PACK)
+            if grp not in res:
+                res[grp] = work.tile([P, PACK, E], F32, name="res", tag="res", bufs=3)
+            if on_vector:
+                nc.vector.tensor_scalar(out=res[grp][:, t, :], in0=u_bank[i][:], scalar1=rs[i][:], scalar2=None,
+                                        op0=ALU.mult)
+            else:
+                nc.scalar.activation(out=res[grp][:, t, :], in_=u_bank[i][:], func=ACT.Copy, scale=rs[i][:])
+            nc.sync.dma_start(out=rows(out_0, grp)[:, t, :], in_=res[grp][:, t, :])
+
+        def res_piece(grp, c, engine):
+            if grp not in res_il:
+                res_il[grp] = work.tile([P, E, PACK], BF16, name="res_il", tag="res_il", bufs=3, align_bytes=64)
+            cols = slice(P * c, P * (c + 1))
+            dst = res_il[grp][:, cols, :]
+            src = res[grp][:, :, cols].rearrange("p t n -> p n t")
+            if engine == "gpsimd":
+                gpsimd_move(dst, src)
+            elif engine == "vector":
+                nc.vector.tensor_copy(out=dst, in_=src)
+            else:
+                nc.scalar.copy(out=dst, in_=src)
+
+        def res_quant(grp):
+            codes, scales = quantize(work, "res", flat(res_il[grp][:]), 4)
+            nc.sync.dma_start(out=out_1[grp].rearrange("p m t -> p (m t)").bitcast(I32), in_=codes[:].bitcast(I32))
+            for quad in range(4):
+                nc.sync.dma_start(out=out_2[grp, PACK * quad : PACK * (quad + 1), :].bitcast(I32),
+                                  in_=scales[32 * quad : 32 * quad + PACK, :].bitcast(I32))
+
+        def v_piece(n):
+            h, c = divmod(n, 4)
+            cols = slice(P * c, P * (c + 1))
+            gpsimd_move(v_il[h][:, cols, :], v_sb[h][:, :, cols].rearrange("p t n -> p n t"))
+
+        for h in range(2):
+            b = spread(kt_f[:, PACK * h : PACK * (h + 1)], "S%d" % h)
+            nc.scalar.copy(out=kt_row[:, BANK * h : BANK * (h + 1)], in_=b[:])
+        kb = [turn_pair(k_sb[0][:, 0:2, :], "T0"), turn_pair(k_sb[0][:, 2:4, :], "T1")]
+        q_turn(0, "Q0")
+        kb += [turn_pair(k_sb[1][:, 0:2, :], "U0"), turn_pair(k_sb[1][:, 2:4, :], "U1")]
+        half = 2 * PACK * P
+        pair_out(True, k_il[0][:, 0:half], kb[0])
+        pair_out(False, k_il[0][:, half : 2 * half], kb[1])
+        q_out(0, True)
+        k_q[0] = quantize(keep, "k0", k_il[0][:], 1)
+        pair_out(True, k_il[1][:, 0:half], kb[2])
+        pair_out(False, k_il[1][:, half : 2 * half], kb[3])
+        q_quant(0)
+        scores(0, 0)
+        k_q[1] = quantize(keep, "k1", k_il[1][:], 1)
+        scores(0, 1)
+        q_turn(1, "X")
+        logits(0, 0)
+        logits(0, 1)
+        scores(1, 0)
+        scores(1, 1)
+        q_out(1, True)
+
+        vsq = keep.tile([P, 2 * PACK], F32, name="vsq")
+        vs_bank = []
+        for h in range(2):
+            c = slice(PACK * h, PACK * (h + 1))
+            for t in range(PACK):
+                j = PACK * h + t
+                nc.scalar.activation(out=junk[:], in_=v_sb[h][:, t, :], func=ACT.Square, scale=g16[:, j : j + 1],
+                                     accum_out=vsq[:, j : j + 1])
+            lift = stat.tile([P, PACK], F32, name="lift", tag="lift")
+            inv = stat.tile([P, PACK], F32, name="inv", tag="inv")
+            vs = stat.tile([P, PACK], F32, name="vs", tag="vs")
+            nc.gpsimd.tensor_scalar(out=lift[:], in0=vsq[:, c], scalar1=1.0, scalar2=1.0, op0=ALU.add, op1=ALU.mult)
+            nc.gpsimd.tensor_tensor(out=inv[:], in0=lift[:], in1=minus_half[:], op=ALU.pow)
+            nc.gpsimd.tensor_tensor(out=vs[:], in0=lift[:], in1=inv[:], op=ALU.mult)
+            nc.gpsimd.tensor_tensor(out=gv[:, c], in0=flat(g_sb[:])[:, c], in1=inv[:], op=ALU.mult)
+            vs_bank.append(spread(vs, "U%d" % h))
+
+        last = TILES - 1
+        for i in range(last):
+            nxt, phase = 2 * (i // 4 + 1), i % 4
+            has_next = nxt < TILES // 2
+            if has_next and phase in (1, 2):
+                q_quant(nxt + phase - 1)
+            if i in (2, 3):
+                v_q[i - 2] = quantize(keep, "v%d" % (i - 2), flat(v_il[i - 2][:]), 1)
+            if i == 13:
+                res_quant(0)
+            if i >= 4:
+                pg_quant(i - 4)
+            if i >= 2:
+                turn(i - 2)
+            if i >= 4:
+                values(i - 4, "U%d" % (i % 2))
+            if has_next and phase in (0, 1):
+                q_turn(nxt + phase, ("Q0", "X")[phase])
+            if i >= 3:
+                interleave(i - 3, 0)
+            if i >= 5:
+                root(i - 5)
+            if i >= 3:
+                interleave(i - 3, 1)
+            if i >= 9:
+                res_piece((i - 9) // 4, (i - 9) % 4, "gpsimd")
+            if i < 2:
+                for n in range(4):
+                    v_piece(4 * i + n)
+            row_max(i)
+            if i == 0:
+                q_quant(1)
+            if i >= 1:
+                recip(i - 1)
+            logits(i + 1, 0)
+            logits(i + 1, 1)
+            if i >= 1:
+                weigh(i - 1)
+            if i == 0:
+                nc.scalar.copy(out=vs_row[:, 0:BANK], in_=vs_bank[0][:])
+            if i >= 2:
+                gain_rows(i - 2)
+            exponent(i)
+            if i == 0:
+                nc.scalar.copy(out=vs_row[:, BANK : 2 * BANK], in_=vs_bank[1][:])
+            if i >= 5:
+                finish(i - 5, False)
+            if i >= 4:
+                square_sum(i - 4)
+            if has_next and phase in (0, 1):
+                q_out(nxt + phase, False)
+            if i + 2 <= last:
+                scores(i + 2, 0)
+                scores(i + 2, 1)
+
+        pg_quant(11)
+        turn(13)
+        values(11, "U1")
+        root(10)
+        interleave(12, 0)
+        interleave(12, 1)
+        row_max(15)
+        recip(14)
+        weigh(14)
+        finish(10, False)
+        exponent(15)
+        gain_rows(13)
+        pg_quant(12)
+        turn(14, ("Q0", "X"))
+        values(12, "S0")
+        recip(15)
+        weigh(15)
+        interleave(13, 0)
+        interleave(13, 1)
+        gain_direct(14, 0)
+        gain_direct(14, 1)
+        turn(15)
+        square_sum(11)
+        square_sum(12)
+        root(11)
+        root(12)
+        finish(11, False)
+        finish(12, False)
+        gain_direct(15, 0)
+        pg_quant(14)
+        gain_direct(15, 1)
+        pg_quant(13)
+        pg_quant(15)
+        values(14, "S1")
+        values(13, "U0")
+        values(15, "Q0")
+        res_piece(1, 2, "gpsimd")
+        res_piece(1, 3, "gpsimd")
+        square_sum(14)
+        square_sum(13)
+        square_sum(15)
+        root(14)
+        res_piece(2, 0, "gpsimd")
+        root(13)
+        res_piece(2, 1, "gpsimd")
+        root(15)
+        res_quant(1)
+        finish(14, True)
+        finish(13, True)
+        finish(15, True)
+        res_piece(2, 2, "scalar")
+        res_piece(2, 3, "scalar")
+        res_piece(3, 0, "vector")
+        res_piece(3, 1, "vector")
+        res_piece(3, 2, "vector")
+        res_piece(3, 3, "scalar")
+        res_quant(2)
+        res_quant(3)

@@ -21,6 +21,7 @@ BANK = 512
 TILES = N // P
 RADIUS = 16.0
 BETA = 2.0
+GSHARE = 64
 
 
 def tile_lorentzcentroidaggregation_x1_kernel(tc, q, qt, k, kt, v, g, out_0, out_1, out_2):
@@ -38,42 +39,64 @@ def tile_lorentzcentroidaggregation_x1_kernel(tc, q, qt, k, kt, v, g, out_0, out
         def flat(ap3):
             return ap3.rearrange("p a b -> p (a b)")
 
-        kt_sb = keep.tile([P, 2, PACK], BF16, name="kt_sb")
-        qt_sb = keep.tile([P, 4, PACK], BF16, name="qt_sb")
-        g_sb = keep.tile([P, 2, PACK], BF16, name="g_sb")
-        nc.scalar.dma_start(out=kt_sb[:], in_=kt.rearrange("(h p t) -> p h t", p=P, t=PACK))
-        nc.scalar.dma_start(out=qt_sb[:], in_=qt.rearrange("(h p t) -> p h t", p=P, t=PACK))
-        nc.scalar.dma_start(out=g_sb[:], in_=g.rearrange("(h p t) -> p h t", p=P, t=PACK))
+        vec_rows = keep.tile([P, BANK], BF16, name="vec_rows")
+        nc.vector.memset(vec_rows[:].bitcast(I32), 0)
+        nc.scalar.dma_start(out=vec_rows[0:4, :], in_=qt.rearrange("(h n) -> h n", n=BANK))
+        nc.scalar.dma_start(out=vec_rows[4:6, :], in_=kt.rearrange("(h n) -> h n", n=BANK))
+        nc.scalar.dma_start(out=vec_rows[6:8, :], in_=g.rearrange("(h n) -> h n", n=BANK))
 
         def rows(src, h):
             return src[BANK * h : BANK * (h + 1), :].rearrange("(p t) d -> p t d", t=PACK)
 
-        k_sb = [keep.tile([P, PACK, D], BF16, name="k_sb%d" % h) for h in range(2)]
+        k_sb = [keep.tile([P, 2, D], BF16, name="k_sb%d" % j) for j in range(4)]
         v_sb = [keep.tile([P, PACK, E], BF16, name="v_sb%d" % h) for h in range(2)]
         q_sb = [keep.tile([P, 2, D], BF16, name="q_sb%d" % j) for j in range(TILES // 2)]
 
         def load_q(j):
             nc.sync.dma_start(out=q_sb[j][:], in_=rows(q, j // 2)[:, 2 * (j % 2) : 2 * (j % 2) + 2, :])
 
-        nc.sync.dma_start(out=k_sb[0][:], in_=rows(k, 0))
+        def load_k(j):
+            nc.sync.dma_start(out=k_sb[j][:], in_=rows(k, j // 2)[:, 2 * (j % 2) : 2 * (j % 2) + 2, :])
+
+        load_k(0)
+        load_k(1)
         load_q(0)
-        nc.sync.dma_start(out=k_sb[1][:], in_=rows(k, 1))
+        load_k(2)
+        load_k(3)
         nc.sync.dma_start(out=v_sb[0][:], in_=rows(v, 0))
+        load_q(1)
         nc.sync.dma_start(out=v_sb[1][:], in_=rows(v, 1))
-        for j in range(1, TILES // 2):
+        for j in range(2, TILES // 2):
             load_q(j)
 
         ident = keep.tile([P, P], F32, name="ident")
         make_identity(nc, ident[:])
         minus_half = keep.tile([P, PACK], F32, name="minus_half")
         nc.gpsimd.memset(minus_half[:], -0.5)
-        warm = keep.tile([P, 1], F32, name="warm")
-        nc.scalar.activation(out=warm[:], in_=minus_half[:, 0:1], func=ACT.Exp)
-        kt_f = keep.tile([P, 2 * PACK], F32, name="kt_f")
-        nc.gpsimd.tensor_copy(out=kt_f[:], in_=flat(kt_sb[:]))
+        vec = keep.tile([P, 8, PACK], F32, name="vec")
+        qt_f, g_f = flat(vec[:, 0:4, :]), flat(vec[:, 6:8, :])
+        pick = keep.tile([P, 2], BF16, name="pick")
+        nc.scalar.activation(out=pick[:], in_=ident[:, 4:6], func=ACT.Copy)
         g16 = keep.tile([P, 2 * PACK], F32, name="g16")
-        nc.gpsimd.tensor_scalar(out=g16[:], in0=flat(g_sb[:]), scalar1=1.0 / RADIUS, scalar2=1.0,
-                                op0=ALU.mult, op1=ALU.mult)
+
+        def turn_vectors(tag):
+            b = bank(tag)
+            words = vec_rows[:].bitcast(F32)
+            for u in range(2):
+                nc.tensor.transpose(b[:, P * u : P * (u + 1)], words[:, u : BANK // 2 : 2], ident[:])
+            pairs = b[:, 0 : 2 * P].bitcast(BF16).rearrange("p (u r c) -> p r u c", u=2, c=2)
+            nc.vector.tensor_copy(out=vec[:].rearrange("p r (u c) -> p r u c", u=2), in_=pairs[:, 0:8, :, :])
+            nc.gpsimd.tensor_scalar(out=g16[:], in0=g_f, scalar1=1.0 / RADIUS, scalar2=1.0,
+                                    op0=ALU.mult, op1=ALU.mult)
+
+        def kt_spread(h):
+            b = bank("S%d" % h)
+            nc.tensor.matmul(out=b[:], lhsT=pick[:, h : h + 1].to_broadcast([P, P]),
+                             rhs=vec_rows[:].rearrange("r (p t) -> r t p", t=PACK), start=True, stop=True)
+            kt_bank[h] = b
+
+        def kt_out(h):
+            nc.scalar.copy(out=kt_row[:, BANK * h : BANK * (h + 1)], in_=kt_bank[h][:])
 
         def spread(col4, tag):
             b = bank(tag)
@@ -106,7 +129,6 @@ def tile_lorentzcentroidaggregation_x1_kernel(tc, q, qt, k, kt, v, g, out_0, out
             return codes, scales
 
         kt_row = keep.tile([P, M], F32, name="kt_row")
-        vs_row = keep.tile([P, M], F32, name="vs_row")
         gv = keep.tile([P, 2 * PACK], F32, name="gv")
         k_il = [keep.tile([P, PACK * BANK], BF16, name="k_il%d" % h, align_bytes=64) for h in range(2)]
         v_il = [keep.tile([P, E, PACK], BF16, name="v_il%d" % h, align_bytes=64) for h in range(2)]
@@ -115,17 +137,17 @@ def tile_lorentzcentroidaggregation_x1_kernel(tc, q, qt, k, kt, v, g, out_0, out
         k_q, v_q, q_q, q_bank, q_il = {}, {}, {}, {}, {}
         s_bank, x, bias, e, z, rz, w, ut, t_bank = {}, {}, {}, {}, {}, {}, {}, {}, {}
         pg_rows, pg_il, pg_q, u_bank, ss, rs = {}, {}, {}, {}, {}, {}
-        res, res_il = {}, {}
+        res, res_il, ut2, gap, vs_bank, k_bank, kt_bank = {}, {}, {}, {}, {}, {}, {}
 
         def q_turn(j, tag):
             q_bank[j] = turn_pair(q_sb[j], tag)
 
         def q_out(j, on_vector):
-            q_il[j] = work.tile([P, 2 * PACK * P], BF16, name="q_il", tag="q_il", align_bytes=64)
+            q_il[j] = work.tile([P, 2 * PACK * P], BF16, name="q_il", tag="q_il", bufs=6, align_bytes=64)
             pair_out(on_vector, q_il[j][:], q_bank[j])
 
         def q_quant(j):
-            q_q[j] = quantize(work, "q", q_il[j][:], 3)
+            q_q[j] = quantize(work, "q", q_il[j][:], 8)
 
         def scores(i, h):
             codes, scales = q_q[i // 2]
@@ -136,9 +158,9 @@ def tile_lorentzcentroidaggregation_x1_kernel(tc, q, qt, k, kt, v, g, out_0, out
 
         def logits(i, h):
             if h == 0:
-                x[i] = work.tile([P, M], F32, name="x", tag="x", bufs=3)
+                x[i] = work.tile([P, M], F32, name="x", tag="x", bufs=4)
             c = slice(BANK * h, BANK * (h + 1))
-            nc.vector.scalar_tensor_tensor(out=x[i][:, c], in0=kt_row[:, c], scalar=flat(qt_sb[:])[:, i : i + 1],
+            nc.vector.scalar_tensor_tensor(out=x[i][:, c], in0=kt_row[:, c], scalar=qt_f[:, i : i + 1],
                                            in1=s_bank[i, h][:], op0=ALU.mult, op1=ALU.subtract)
 
         def row_max(i):
@@ -158,9 +180,15 @@ def tile_lorentzcentroidaggregation_x1_kernel(tc, q, qt, k, kt, v, g, out_0, out
 
         def weigh(i):
             w[i] = work.tile([P, M], F32, name="w", tag="w")
-            ut[i] = stat.tile([P, 1], F32, name="ut", tag="ut", bufs=8)
-            nc.vector.scalar_tensor_tensor(out=w[i][:], in0=e[i][:], scalar=rz[i][:], in1=vs_row[:],
-                                           op0=ALU.mult, op1=ALU.mult, accum_out=ut[i][:])
+            ut[i] = stat.tile([P, 2], F32, name="ut", tag="ut")
+            for h in range(2):
+                c = slice(BANK * h, BANK * (h + 1))
+                nc.vector.scalar_tensor_tensor(out=w[i][:, c], in0=e[i][:, c], scalar=rz[i][:], in1=vs_bank[h][:],
+                                               op0=ALU.mult, op1=ALU.mult, accum_out=ut[i][:, h : h + 1])
+
+        def time_square(i):
+            ut2[i] = stat.tile([P, 1], F32, name="ut2", tag="ut2", bufs=8)
+            nc.scalar.activation(out=ut2[i][:], in_=ut[i][:, 0:1], func=ACT.Square, bias=ut[i][:, 1:2])
 
         def turn(i, tags=("T0", "T1")):
             for h in range(2):
@@ -187,7 +215,7 @@ def tile_lorentzcentroidaggregation_x1_kernel(tc, q, qt, k, kt, v, g, out_0, out
 
         def gain_direct(i, h):
             if h == 0:
-                pg_il[i] = work.tile([P, 2, P, PACK], BF16, name="pg_dir", tag="pg_dir", bufs=2, align_bytes=64)
+                pg_il[i] = work.tile([P, 2, P, PACK], BF16, name="pg_dir", tag="pg_dir", bufs=3, align_bytes=64)
             nc.vector.tensor_tensor(
                 out=pg_il[i][:, h, :, :], in0=t_bank[i, h][:].rearrange("p (t n) -> p n t", t=PACK),
                 in1=gv[:, PACK * h : PACK * (h + 1)].unsqueeze(1).to_broadcast([P, P, PACK]), op=ALU.mult)
@@ -209,17 +237,27 @@ def tile_lorentzcentroidaggregation_x1_kernel(tc, q, qt, k, kt, v, g, out_0, out
             nc.scalar.activation(out=junk[:], in_=u_bank[i][:], func=ACT.Square, scale=1.0 / RADIUS,
                                  accum_out=ss[i][:])
 
-        def root(i):
-            gap = stat.tile([P, 1], F32, name="gap", tag="gap")
+        def root_gap(i):
+            gap[i] = stat.tile([P, 1], F32, name="gap", tag="gap")
+            nc.gpsimd.tensor_scalar(out=gap[i][:], in0=ss[i][:], scalar1=-1.0, scalar2=ut2[i][:],
+                                    op0=ALU.mult, op1=ALU.add)
+
+        def root_gap_scalar(i):
+            gap[i] = stat.tile([P, 1], F32, name="gap", tag="gap")
+            nc.scalar.activation(out=gap[i][:], in_=ss[i][:], func=ACT.Identity, scale=-1.0, bias=ut2[i][:])
+
+        def root_pow(i):
             rs[i] = stat.tile([P, 1], F32, name="rs", tag="rs")
-            nc.gpsimd.tensor_scalar(out=gap[:], in0=ut[i][:], scalar1=ut[i][:], scalar2=ss[i][:],
-                                    op0=ALU.mult, op1=ALU.subtract)
-            nc.gpsimd.tensor_tensor(out=rs[i][:], in0=gap[:], in1=minus_half[:, 0:1], op=ALU.pow)
+            nc.gpsimd.tensor_tensor(out=rs[i][:], in0=gap[i][:], in1=minus_half[:, 0:1], op=ALU.pow)
+
+        def root(i):
+            root_gap(i)
+            root_pow(i)
 
         def finish(i, on_vector):
             grp, t = divmod(i, PACK)
             if grp not in res:
-                res[grp] = work.tile([P, PACK, E], F32, name="res", tag="res", bufs=3)
+                res[grp] = work.tile([P, PACK, E], F32, name="res", tag="res", bufs=4)
             if on_vector:
                 nc.vector.tensor_scalar(out=res[grp][:, t, :], in0=u_bank[i][:], scalar1=rs[i][:], scalar2=None,
                                         op0=ALU.mult)
@@ -227,12 +265,13 @@ def tile_lorentzcentroidaggregation_x1_kernel(tc, q, qt, k, kt, v, g, out_0, out
                 nc.scalar.activation(out=res[grp][:, t, :], in_=u_bank[i][:], func=ACT.Copy, scale=rs[i][:])
             nc.sync.dma_start(out=rows(out_0, grp)[:, t, :], in_=res[grp][:, t, :])
 
-        def res_piece(grp, c, engine):
+        def res_piece(grp, lo, hi, engine):
             if grp not in res_il:
-                res_il[grp] = work.tile([P, E, PACK], BF16, name="res_il", tag="res_il", bufs=3, align_bytes=64)
-            cols = slice(P * c, P * (c + 1))
-            dst = res_il[grp][:, cols, :]
-            src = res[grp][:, :, cols].rearrange("p t n -> p n t")
+                res_il[grp] = work.tile([P, E, PACK], BF16, name="res_il", tag="res_il", bufs=4, align_bytes=64)
+            cols = slice(lo, hi)
+            move(res_il[grp][:, cols, :], res[grp][:, :, cols].rearrange("p t n -> p n t"), engine)
+
+        def move(dst, src, engine):
             if engine == "gpsimd":
                 gpsimd_move(dst, src)
             elif engine == "vector":
@@ -247,38 +286,29 @@ def tile_lorentzcentroidaggregation_x1_kernel(tc, q, qt, k, kt, v, g, out_0, out
                 nc.sync.dma_start(out=out_2[grp, PACK * quad : PACK * (quad + 1), :].bitcast(I32),
                                   in_=scales[32 * quad : 32 * quad + PACK, :].bitcast(I32))
 
-        def v_piece(n):
-            h, c = divmod(n, 4)
-            cols = slice(P * c, P * (c + 1))
-            gpsimd_move(v_il[h][:, cols, :], v_sb[h][:, :, cols].rearrange("p t n -> p n t"))
+        def v_piece(h, lo, hi, engine):
+            move(v_il[h][:, lo:hi, :], v_sb[h][:, :, lo:hi].rearrange("p t n -> p n t"), engine)
 
-        for h in range(2):
-            b = spread(kt_f[:, PACK * h : PACK * (h + 1)], "S%d" % h)
-            nc.scalar.copy(out=kt_row[:, BANK * h : BANK * (h + 1)], in_=b[:])
-        kb = [turn_pair(k_sb[0][:, 0:2, :], "T0"), turn_pair(k_sb[0][:, 2:4, :], "T1")]
-        q_turn(0, "Q0")
-        kb += [turn_pair(k_sb[1][:, 0:2, :], "U0"), turn_pair(k_sb[1][:, 2:4, :], "U1")]
-        half = 2 * PACK * P
-        pair_out(True, k_il[0][:, 0:half], kb[0])
-        pair_out(False, k_il[0][:, half : 2 * half], kb[1])
-        q_out(0, True)
-        k_q[0] = quantize(keep, "k0", k_il[0][:], 1)
-        pair_out(True, k_il[1][:, 0:half], kb[2])
-        pair_out(False, k_il[1][:, half : 2 * half], kb[3])
-        q_quant(0)
-        scores(0, 0)
-        k_q[1] = quantize(keep, "k1", k_il[1][:], 1)
-        scores(0, 1)
-        q_turn(1, "X")
-        logits(0, 0)
-        logits(0, 1)
-        scores(1, 0)
-        scores(1, 1)
-        q_out(1, True)
+        def v_quant(h):
+            v_q[h] = quantize(keep, "v%d" % h, flat(v_il[h][:]), 1)
+
+        def k_turn(j, tag):
+            k_bank[j] = turn_pair(k_sb[j], tag)
+
+        def k_out(j, on_vector):
+            half = 2 * PACK * P
+            pair_out(on_vector, k_il[j // 2][:, half * (j % 2) : half * (j % 2 + 1)], k_bank[j])
+
+        def k_quant(h):
+            k_q[h] = quantize(keep, "k%d" % h, k_il[h][:], 1)
+
+        def vs_spread(h):
+            vs_bank[h] = spread(vs[h], "V%d" % h)
 
         vsq = keep.tile([P, 2 * PACK], F32, name="vsq")
-        vs_bank = []
-        for h in range(2):
+        vs = {}
+
+        def value_time(h):
             c = slice(PACK * h, PACK * (h + 1))
             for t in range(PACK):
                 j = PACK * h + t
@@ -286,123 +316,197 @@ def tile_lorentzcentroidaggregation_x1_kernel(tc, q, qt, k, kt, v, g, out_0, out
                                      accum_out=vsq[:, j : j + 1])
             lift = stat.tile([P, PACK], F32, name="lift", tag="lift")
             inv = stat.tile([P, PACK], F32, name="inv", tag="inv")
-            vs = stat.tile([P, PACK], F32, name="vs", tag="vs")
+            vs[h] = stat.tile([P, PACK], F32, name="vs", tag="vs")
             nc.gpsimd.tensor_scalar(out=lift[:], in0=vsq[:, c], scalar1=1.0, scalar2=1.0, op0=ALU.add, op1=ALU.mult)
             nc.gpsimd.tensor_tensor(out=inv[:], in0=lift[:], in1=minus_half[:], op=ALU.pow)
-            nc.gpsimd.tensor_tensor(out=vs[:], in0=lift[:], in1=inv[:], op=ALU.mult)
-            nc.gpsimd.tensor_tensor(out=gv[:, c], in0=flat(g_sb[:])[:, c], in1=inv[:], op=ALU.mult)
-            vs_bank.append(spread(vs, "U%d" % h))
+            nc.gpsimd.tensor_tensor(out=vs[h][:], in0=lift[:], in1=inv[:], op=ALU.mult)
+            nc.gpsimd.tensor_tensor(out=gv[:, c], in0=g_f[:, c], in1=inv[:], op=ALU.mult)
 
-        last = TILES - 1
-        for i in range(last):
-            nxt, phase = 2 * (i // 4 + 1), i % 4
-            has_next = nxt < TILES // 2
-            if has_next and phase in (1, 2):
-                q_quant(nxt + phase - 1)
+        k_turn(0, "T0")
+        k_turn(1, "T1")
+        turn_vectors("V1")
+        k_out(1, True)
+        kt_spread(0)
+        kt_spread(1)
+        q_turn(0, "U0")
+        kt_out(1)
+        q_out(0, False)
+        kt_out(0)
+        k_out(0, True)
+        k_turn(3, "V0")
+        k_quant(0)
+        k_turn(2, "U1")
+        q_quant(0)
+        k_out(2, True)
+        q_turn(1, "T0")
+        scores(0, 0)
+        k_out(3, False)
+        value_time(0)
+        k_quant(1)
+        v_piece(1, 0, 128, "gpsimd")
+        scores(0, 1)
+        scores(1, 0)
+        q_out(1, False)
+        logits(0, 0)
+        logits(0, 1)
+        q_turn(2, "T1")
+        logits(1, 0)
+        row_max(0)
+        value_time(1)
+        exponent(0)
+        scores(1, 1)
+        q_out(2, False)
+        v_piece(1, 256, 384, "gpsimd")
+        v_piece(0, 0, 256, "scalar")
+        q_quant(1)
+        scores(2, 0)
+        vs_spread(0)
+        scores(2, 1)
+        logits(1, 1)
+        row_max(1)
+        v_piece(1, 384, 512, "gpsimd")
+        logits(2, 0)
+        scores(3, 0)
+        logits(2, 1)
+        scores(3, 1)
+        recip(0)
+        q_quant(2)
+        vs_spread(1)
+        scores(4, 0)
+        logits(3, 0)
+        v_piece(0, 256, 512, "scalar")
+        logits(3, 1)
+        exponent(1)
+        v_piece(1, 128, 256, "scalar")
+        weigh(0)
+        row_max(2)
+        scores(4, 1)
+
+        q_copy_at = {2: (3, 4), 3: (5, 6), 4: (7,)}
+        q_quant_at = {3: 3, 4: 4, 5: 5, 6: 6, 7: 7}
+        for i in range(2, 14):
+            if i in q_quant_at:
+                q_quant(q_quant_at[i])
             if i in (2, 3):
-                v_q[i - 2] = quantize(keep, "v%d" % (i - 2), flat(v_il[i - 2][:]), 1)
-            if i == 13:
-                res_quant(0)
+                v_quant(i - 2)
             if i >= 4:
                 pg_quant(i - 4)
             if i >= 2:
                 turn(i - 2)
             if i >= 4:
                 values(i - 4, "U%d" % (i % 2))
-            if has_next and phase in (0, 1):
-                q_turn(nxt + phase, ("Q0", "X")[phase])
             if i >= 3:
                 interleave(i - 3, 0)
             if i >= 5:
-                root(i - 5)
+                root_gap(i - 5)
             if i >= 3:
                 interleave(i - 3, 1)
+            if i >= 5:
+                root_pow(i - 5)
             if i >= 9:
-                res_piece((i - 9) // 4, (i - 9) % 4, "gpsimd")
-            if i < 2:
-                for n in range(4):
-                    v_piece(4 * i + n)
-            row_max(i)
-            if i == 0:
-                q_quant(1)
+                res_piece(0, GSHARE * (i - 9), min(E, GSHARE * (i - 8)), "gpsimd")
+            row_max(i + 1)
             if i >= 1:
                 recip(i - 1)
-            logits(i + 1, 0)
-            logits(i + 1, 1)
+            logits(i + 2, 0)
+            logits(i + 2, 1)
             if i >= 1:
                 weigh(i - 1)
-            if i == 0:
-                nc.scalar.copy(out=vs_row[:, 0:BANK], in_=vs_bank[0][:])
             if i >= 2:
                 gain_rows(i - 2)
+                time_square(i - 2)
             exponent(i)
-            if i == 0:
-                nc.scalar.copy(out=vs_row[:, BANK : 2 * BANK], in_=vs_bank[1][:])
+            for n, j in enumerate(q_copy_at.get(i, ())):
+                q_turn(j, "T%d" % n)
+                q_out(j, False)
             if i >= 5:
                 finish(i - 5, False)
             if i >= 4:
                 square_sum(i - 4)
-            if has_next and phase in (0, 1):
-                q_out(nxt + phase, False)
-            if i + 2 <= last:
-                scores(i + 2, 0)
-                scores(i + 2, 1)
+            if i + 3 < TILES:
+                scores(i + 3, 0)
+                scores(i + 3, 1)
 
-        pg_quant(11)
-        turn(13)
-        values(11, "U1")
-        root(10)
-        interleave(12, 0)
-        interleave(12, 1)
+        interleave(11, 0)
+        exponent(14)
+        turn(12)
+        pg_quant(10)
+        root_gap_scalar(9)
+        recip(13)
         row_max(15)
+        values(10, "U0")
+        gain_rows(12)
+        weigh(13)
+        interleave(11, 1)
+        turn(13, ("S0", "S1"))
+        root_pow(9)
+        res_piece(0, 320, 416, "gpsimd")
         recip(14)
-        weigh(14)
-        finish(10, False)
         exponent(15)
-        gain_rows(13)
-        pg_quant(12)
-        turn(14, ("Q0", "X"))
-        values(12, "S0")
+        pg_quant(11)
+        weigh(14)
+        gain_direct(13, 0)
+        turn(14)
+        finish(9, False)
+        square_sum(10)
         recip(15)
+        time_square(12)
+        time_square(14)
+        values(11, "U1")
+        gain_direct(13, 1)
+        interleave(12, 0)
         weigh(15)
-        interleave(13, 0)
-        interleave(13, 1)
-        gain_direct(14, 0)
-        gain_direct(14, 1)
-        turn(15)
-        square_sum(11)
-        square_sum(12)
-        root(11)
-        root(12)
-        finish(11, False)
-        finish(12, False)
-        gain_direct(15, 0)
-        pg_quant(14)
-        gain_direct(15, 1)
+        interleave(12, 1)
         pg_quant(13)
-        pg_quant(15)
-        values(14, "S1")
-        values(13, "U0")
-        values(15, "Q0")
-        res_piece(1, 2, "gpsimd")
-        res_piece(1, 3, "gpsimd")
-        square_sum(14)
+        root_gap_scalar(10)
+        root_pow(10)
+        pg_quant(12)
+        square_sum(11)
+        gain_direct(14, 0)
+        turn(15, ("S0", "S1"))
+        finish(10, False)
+        root_gap(11)
+        root_pow(11)
+        values(12, "U0")
+        gain_direct(14, 1)
+        gain_direct(15, 0)
+        res_piece(1, 0, 128, "scalar")
+        res_piece(0, 416, 512, "scalar")
+        square_sum(12)
+        res_piece(1, 128, 256, "vector")
+        pg_quant(14)
+        finish(11, False)
+        values(13, "V0")
+        values(14, "V1")
+        gain_direct(15, 1)
+        time_square(13)
+        root_gap_scalar(12)
         square_sum(13)
-        square_sum(15)
-        root(14)
-        res_piece(2, 0, "gpsimd")
-        root(13)
-        res_piece(2, 1, "gpsimd")
-        root(15)
-        res_quant(1)
-        finish(14, True)
+        root_pow(12)
+        pg_quant(15)
+        values(15, "T0")
+        square_sum(14)
+        res_piece(2, 0, 128, "vector")
+        root_gap_scalar(13)
+        time_square(15)
+        root_pow(13)
+        res_piece(1, 256, 384, "scalar")
+        root_gap_scalar(14)
+        res_piece(1, 384, 512, "vector")
+        finish(12, True)
+        res_quant(0)
         finish(13, True)
-        finish(15, True)
-        res_piece(2, 2, "scalar")
-        res_piece(2, 3, "scalar")
-        res_piece(3, 0, "vector")
-        res_piece(3, 1, "vector")
-        res_piece(3, 2, "vector")
-        res_piece(3, 3, "scalar")
+        square_sum(15)
+        res_piece(2, 256, 384, "scalar")
+        root_pow(14)
+        res_piece(2, 128, 256, "vector")
+        root_gap_scalar(15)
+        res_piece(2, 384, 512, "scalar")
+        finish(14, True)
+        res_quant(1)
+        root_pow(15)
+        finish(15, False)
         res_quant(2)
+        res_piece(3, 384, 512, "scalar")
+        res_piece(3, 0, 384, "vector")
         res_quant(3)

from contextlib import ExitStack

import concourse.mybir as mybir
from concourse.masks import make_identity

N, M, D, E = 2048, 1024, 512, 512
FLOPS = 2 * N * M * D + 2 * N * M * E

F32 = mybir.dt.float32
BF16 = mybir.dt.bfloat16
I32 = mybir.dt.int32
U32 = mybir.dt.uint32
U8 = mybir.dt.uint8
FP8X4 = mybir.dt.float8_e4m3fn_x4
ALU = mybir.AluOpType
ACT = mybir.ActivationFunctionType

P = 128
PACK = 4
BANK = 512
TILES = N // P
RADIUS = 16.0
BETA = 2.0
GSHARE = 64


def tile_lorentzcentroidaggregation_x1_kernel(tc, q, qt, k, kt, v, g, out_0, out_1, out_2):
    nc = tc.nc
    with ExitStack() as ctx:
        keep = ctx.enter_context(tc.tile_pool(name="keep", bufs=1))
        work = ctx.enter_context(tc.tile_pool(name="work", bufs=2))
        stat = ctx.enter_context(tc.tile_pool(name="stat", bufs=4))
        psum = ctx.enter_context(tc.psum_pool(name="psum", bufs=1))
        ctx.enter_context(tc.manual_schedule())

        def bank(tag):
            return psum.tile([P, BANK], F32, name=tag, tag=tag)

        def flat(ap3):
            return ap3.rearrange("p a b -> p (a b)")

        vec_rows = keep.tile([P, BANK], BF16, name="vec_rows")
        nc.vector.memset(vec_rows[:].bitcast(I32), 0)
        nc.scalar.dma_start(out=vec_rows[0:4, :], in_=qt.rearrange("(h n) -> h n", n=BANK))
        nc.scalar.dma_start(out=vec_rows[4:6, :], in_=kt.rearrange("(h n) -> h n", n=BANK))
        nc.scalar.dma_start(out=vec_rows[6:8, :], in_=g.rearrange("(h n) -> h n", n=BANK))

        def rows(src, h):
            return src[BANK * h : BANK * (h + 1), :].rearrange("(p t) d -> p t d", t=PACK)

        k_sb = [keep.tile([P, 2, D], BF16, name="k_sb%d" % j) for j in range(4)]
        v_sb = [keep.tile([P, PACK, E], BF16, name="v_sb%d" % h) for h in range(2)]
        q_sb = [keep.tile([P, 2, D], BF16, name="q_sb%d" % j) for j in range(TILES // 2)]

        def load_q(j):
            nc.sync.dma_start(out=q_sb[j][:], in_=rows(q, j // 2)[:, 2 * (j % 2) : 2 * (j % 2) + 2, :])

        def load_k(j):
            nc.sync.dma_start(out=k_sb[j][:], in_=rows(k, j // 2)[:, 2 * (j % 2) : 2 * (j % 2) + 2, :])

        load_k(0)
        load_k(1)
        load_q(0)
        load_k(2)
        load_k(3)
        nc.sync.dma_start(out=v_sb[0][:], in_=rows(v, 0))
        load_q(1)
        nc.sync.dma_start(out=v_sb[1][:], in_=rows(v, 1))
        for j in range(2, TILES // 2):
            load_q(j)

        ident = keep.tile([P, P], F32, name="ident")
        make_identity(nc, ident[:])
        minus_half = keep.tile([P, PACK], F32, name="minus_half")
        nc.gpsimd.memset(minus_half[:], -0.5)
        vec = keep.tile([P, 8, PACK], F32, name="vec")
        qt_f, g_f = flat(vec[:, 0:4, :]), flat(vec[:, 6:8, :])
        pick = keep.tile([P, 2], BF16, name="pick")
        nc.scalar.activation(out=pick[:], in_=ident[:, 4:6], func=ACT.Copy)
        g16 = keep.tile([P, 2 * PACK], F32, name="g16")

        def turn_vectors(tag):
            b = bank(tag)
            words = vec_rows[:].bitcast(F32)
            for u in range(2):
                nc.tensor.transpose(b[:, P * u : P * (u + 1)], words[:, u : BANK // 2 : 2], ident[:])
            pairs = b[:, 0 : 2 * P].bitcast(BF16).rearrange("p (u r c) -> p r u c", u=2, c=2)
            nc.vector.tensor_copy(out=vec[:].rearrange("p r (u c) -> p r u c", u=2), in_=pairs[:, 0:8, :, :])
            nc.gpsimd.tensor_scalar(out=g16[:], in0=g_f, scalar1=1.0 / RADIUS, scalar2=1.0,
                                    op0=ALU.mult, op1=ALU.mult)

        def kt_spread(h):
            b = bank("S%d" % h)
            nc.tensor.matmul(out=b[:], lhsT=pick[:, h : h + 1].to_broadcast([P, P]),
                             rhs=vec_rows[:].rearrange("r (p t) -> r t p", t=PACK), start=True, stop=True)
            kt_bank[h] = b

        def kt_out(h):
            nc.scalar.copy(out=kt_row[:, BANK * h : BANK * (h + 1)], in_=kt_bank[h][:])

        def spread(col4, tag):
            b = bank(tag)
            for t in range(PACK):
                nc.tensor.transpose(b[:, P * t : P * (t + 1)], col4[:, t : t + 1].to_broadcast([P, P]), ident[:])
            return b

        def turn_pair(src, tag):
            b = bank(tag)
            for s in range(2):
                words = src[:, s, :].bitcast(F32)
                for u in range(2):
                    c = P * (2 * s + u)
                    nc.tensor.transpose(b[:, c : c + P], words[:, u : D // 2 : 2], ident[:])
            return b

        def pair_out(on_vector, dst, b):
            src = b[:].rearrange("p (s u n) -> p s n u", s=2, u=2)
            dstw = dst.bitcast(F32).rearrange("p (s n u) -> p s n u", s=2, u=2)
            if on_vector:
                nc.vector.tensor_copy(out=dstw, in_=src)
            else:
                nc.scalar.copy(out=dstw, in_=src)

        def quantize(pool, name, src, bufs):
            width = src.shape[1] // PACK
            codes = pool.tile([P, width], U32, name=name + "_c", tag=name + "_c", bufs=bufs, align_bytes=64)
            scales = pool.tile([P, width], U8, name=name + "_s", tag=name + "_s", bufs=bufs, align_bytes=64)
            nc.vector.quantize_mx(out=codes[:].bitcast(FP8X4), scales=scales[:], in_=src)
            return codes, scales

        kt_row = keep.tile([P, M], F32, name="kt_row")
        gv = keep.tile([P, 2 * PACK], F32, name="gv")
        k_il = [keep.tile([P, PACK * BANK], BF16, name="k_il%d" % h, align_bytes=64) for h in range(2)]
        v_il = [keep.tile([P, E, PACK], BF16, name="v_il%d" % h, align_bytes=64) for h in range(2)]
        junk = keep.tile([P, BANK], BF16, name="junk")

        k_q, v_q, q_q, q_bank, q_il = {}, {}, {}, {}, {}
        s_bank, x, bias, e, z, rz, w, ut, t_bank = {}, {}, {}, {}, {}, {}, {}, {}, {}
        pg_rows, pg_il, pg_q, u_bank, ss, rs = {}, {}, {}, {}, {}, {}
        res, res_il, ut2, gap, vs_bank, k_bank, kt_bank = {}, {}, {}, {}, {}, {}, {}

        def q_turn(j, tag):
            q_bank[j] = turn_pair(q_sb[j], tag)

        def q_out(j, on_vector):
            q_il[j] = work.tile([P, 2 * PACK * P], BF16, name="q_il", tag="q_il", bufs=6, align_bytes=64)
            pair_out(on_vector, q_il[j][:], q_bank[j])

        def q_quant(j):
            q_q[j] = quantize(work, "q", q_il[j][:], 8)

        def scores(i, h):
            codes, scales = q_q[i // 2]
            c = slice(P * (i % 2), P * (i % 2 + 1))
            s_bank[i, h] = bank("S%d" % h)
            nc.tensor.matmul_mx(out=s_bank[i, h][:], lhsT=codes[:, c].bitcast(FP8X4), lhsT_scale=scales[:, c],
                                rhs=k_q[h][0][:].bitcast(FP8X4), rhs_scale=k_q[h][1][:], start=True, stop=True)

        def logits(i, h):
            if h == 0:
                x[i] = work.tile([P, M], F32, name="x", tag="x", bufs=4)
            c = slice(BANK * h, BANK * (h + 1))
            nc.vector.scalar_tensor_tensor(out=x[i][:, c], in0=kt_row[:, c], scalar=qt_f[:, i : i + 1],
                                           in1=s_bank[i, h][:], op0=ALU.mult, op1=ALU.subtract)

        def row_max(i):
            bias[i] = stat.tile([P, 1], F32, name="bias", tag="bias")
            nc.vector.tensor_scalar(out=x[i][:], in0=x[i][:], scalar1=BETA, scalar2=None,
                                    op0=ALU.mult, op1=ALU.min, accum_out=bias[i][:])

        def exponent(i):
            e[i] = work.tile([P, M], F32, name="e", tag="e", bufs=3)
            z[i] = stat.tile([P, 1], F32, name="z", tag="z")
            nc.scalar.activation(out=e[i][:], in_=x[i][:], func=ACT.Exp, scale=-1.0, bias=bias[i][:],
                                 accum_out=z[i][:])

        def recip(i):
            rz[i] = stat.tile([P, 1], F32, name="rz", tag="rz")
            nc.vector.reciprocal(out=rz[i][:], in_=z[i][:])

        def weigh(i):
            w[i] = work.tile([P, M], F32, name="w", tag="w")
            ut[i] = stat.tile([P, 2], F32, name="ut", tag="ut")
            for h in range(2):
                c = slice(BANK * h, BANK * (h + 1))
                nc.vector.scalar_tensor_tensor(out=w[i][:, c], in0=e[i][:, c], scalar=rz[i][:], in1=vs_bank[h][:],
                                               op0=ALU.mult, op1=ALU.mult, accum_out=ut[i][:, h : h + 1])

        def time_square(i):
            ut2[i] = stat.tile([P, 1], F32, name="ut2", tag="ut2", bufs=8)
            nc.scalar.activation(out=ut2[i][:], in_=ut[i][:, 0:1], func=ACT.Square, bias=ut[i][:, 1:2])

        def turn(i, tags=("T0", "T1")):
            for h in range(2):
                t_bank[i, h] = bank(tags[h])
                for t in range(PACK):
                    c = BANK * h + P * t
                    nc.tensor.transpose(t_bank[i, h][:, P * t : P * (t + 1)], w[i][:, c : c + P], ident[:])

        def gain_rows(i):
            pg_rows[i] = work.tile([P, 2, PACK, P], BF16, name="pg_rows", tag="pg_rows", bufs=3)
            for h in range(2):
                for t in range(PACK):
                    j = PACK * h + t
                    nc.scalar.activation(out=pg_rows[i][:, h, t, :], in_=t_bank[i, h][:, P * t : P * (t + 1)],
                                         func=ACT.Copy, scale=gv[:, j : j + 1])

        def gpsimd_move(dst, src):
            nc.gpsimd.tensor_scalar(out=dst, in0=src, scalar1=1.0, scalar2=1.0, op0=ALU.mult, op1=ALU.mult)

        def interleave(i, h):
            if h == 0:
                pg_il[i] = work.tile([P, 2, P, PACK], BF16, name="pg_il", tag="pg_il", bufs=1, align_bytes=64)
            gpsimd_move(pg_il[i][:, h, :, :], pg_rows[i][:, h, :, :].rearrange("p t n -> p n t"))

        def gain_direct(i, h):
            if h == 0:
                pg_il[i] = work.tile([P, 2, P, PACK], BF16, name="pg_dir", tag="pg_dir", bufs=3, align_bytes=64)
            nc.vector.tensor_tensor(
                out=pg_il[i][:, h, :, :], in0=t_bank[i, h][:].rearrange("p (t n) -> p n t", t=PACK),
                in1=gv[:, PACK * h : PACK * (h + 1)].unsqueeze(1).to_broadcast([P, P, PACK]), op=ALU.mult)

        def pg_quant(i):
            pg_q[i] = quantize(work, "pg", pg_il[i][:].rearrange("p h n t -> p (h n t)"), 3)

        def values(i, tag):
            codes, scales = pg_q[i]
            u_bank[i] = bank(tag)
            for h in range(2):
                c = slice(P * h, P * (h + 1))
                nc.tensor.matmul_mx(out=u_bank[i][:], lhsT=codes[:, c].bitcast(FP8X4), lhsT_scale=scales[:, c],
                                    rhs=v_q[h][0][:].bitcast(FP8X4), rhs_scale=v_q[h][1][:],
                                    start=(h == 0), stop=(h == 1))

        def square_sum(i):
            ss[i] = stat.tile([P, 1], F32, name="ss", tag="ss")
            nc.scalar.activation(out=junk[:], in_=u_bank[i][:], func=ACT.Square, scale=1.0 / RADIUS,
                                 accum_out=ss[i][:])

        def root_gap(i):
            gap[i] = stat.tile([P, 1], F32, name="gap", tag="gap")
            nc.gpsimd.tensor_scalar(out=gap[i][:], in0=ss[i][:], scalar1=-1.0, scalar2=ut2[i][:],
                                    op0=ALU.mult, op1=ALU.add)

        def root_gap_scalar(i):
            gap[i] = stat.tile([P, 1], F32, name="gap", tag="gap")
            nc.scalar.activation(out=gap[i][:], in_=ss[i][:], func=ACT.Identity, scale=-1.0, bias=ut2[i][:])

        def root_pow(i):
            rs[i] = stat.tile([P, 1], F32, name="rs", tag="rs")
            nc.gpsimd.tensor_tensor(out=rs[i][:], in0=gap[i][:], in1=minus_half[:, 0:1], op=ALU.pow)

        def root(i):
            root_gap(i)
            root_pow(i)

        def finish(i, on_vector):
            grp, t = divmod(i, PACK)
            if grp not in res:
                res[grp] = work.tile([P, PACK, E], F32, name="res", tag="res", bufs=4)
            if on_vector:
                nc.vector.tensor_scalar(out=res[grp][:, t, :], in0=u_bank[i][:], scalar1=rs[i][:], scalar2=None,
                                        op0=ALU.mult)
            else:
                nc.scalar.activation(out=res[grp][:, t, :], in_=u_bank[i][:], func=ACT.Copy, scale=rs[i][:])
            nc.sync.dma_start(out=rows(out_0, grp)[:, t, :], in_=res[grp][:, t, :])

        def res_piece(grp, lo, hi, engine):
            if grp not in res_il:
                res_il[grp] = work.tile([P, E, PACK], BF16, name="res_il", tag="res_il", bufs=4, align_bytes=64)
            cols = slice(lo, hi)
            move(res_il[grp][:, cols, :], res[grp][:, :, cols].rearrange("p t n -> p n t"), engine)

        def move(dst, src, engine):
            if engine == "gpsimd":
                gpsimd_move(dst, src)
            elif engine == "vector":
                nc.vector.tensor_copy(out=dst, in_=src)
            else:
                nc.scalar.copy(out=dst, in_=src)

        def res_quant(grp):
            codes, scales = quantize(work, "res", flat(res_il[grp][:]), 4)
            nc.sync.dma_start(out=out_1[grp].rearrange("p m t -> p (m t)").bitcast(I32), in_=codes[:].bitcast(I32))
            for quad in range(4):
                nc.sync.dma_start(out=out_2[grp, PACK * quad : PACK * (quad + 1), :].bitcast(I32),
                                  in_=scales[32 * quad : 32 * quad + PACK, :].bitcast(I32))

        def v_piece(h, lo, hi, engine):
            move(v_il[h][:, lo:hi, :], v_sb[h][:, :, lo:hi].rearrange("p t n -> p n t"), engine)

        def v_quant(h):
            v_q[h] = quantize(keep, "v%d" % h, flat(v_il[h][:]), 1)

        def k_turn(j, tag):
            k_bank[j] = turn_pair(k_sb[j], tag)

        def k_out(j, on_vector):
            half = 2 * PACK * P
            pair_out(on_vector, k_il[j // 2][:, half * (j % 2) : half * (j % 2 + 1)], k_bank[j])

        def k_quant(h):
            k_q[h] = quantize(keep, "k%d" % h, k_il[h][:], 1)

        def vs_spread(h):
            vs_bank[h] = spread(vs[h], "V%d" % h)

        vsq = keep.tile([P, 2 * PACK], F32, name="vsq")
        vs = {}

        def value_time(h):
            c = slice(PACK * h, PACK * (h + 1))
            for t in range(PACK):
                j = PACK * h + t
                nc.scalar.activation(out=junk[:], in_=v_sb[h][:, t, :], func=ACT.Square, scale=g16[:, j : j + 1],
                                     accum_out=vsq[:, j : j + 1])
            lift = stat.tile([P, PACK], F32, name="lift", tag="lift")
            inv = stat.tile([P, PACK], F32, name="inv", tag="inv")
            vs[h] = stat.tile([P, PACK], F32, name="vs", tag="vs")
            nc.gpsimd.tensor_scalar(out=lift[:], in0=vsq[:, c], scalar1=1.0, scalar2=1.0, op0=ALU.add, op1=ALU.mult)
            nc.gpsimd.tensor_tensor(out=inv[:], in0=lift[:], in1=minus_half[:], op=ALU.pow)
            nc.gpsimd.tensor_tensor(out=vs[h][:], in0=lift[:], in1=inv[:], op=ALU.mult)
            nc.gpsimd.tensor_tensor(out=gv[:, c], in0=g_f[:, c], in1=inv[:], op=ALU.mult)

        k_turn(0, "T0")
        k_turn(1, "T1")
        turn_vectors("V1")
        k_out(1, True)
        kt_spread(0)
        kt_spread(1)
        q_turn(0, "U0")
        kt_out(1)
        q_out(0, False)
        kt_out(0)
        k_out(0, True)
        k_turn(3, "V0")
        k_quant(0)
        k_turn(2, "U1")
        q_quant(0)
        k_out(2, True)
        q_turn(1, "T0")
        scores(0, 0)
        k_out(3, False)
        value_time(0)
        k_quant(1)
        v_piece(1, 0, 128, "gpsimd")
        scores(0, 1)
        scores(1, 0)
        q_out(1, False)
        logits(0, 0)
        logits(0, 1)
        q_turn(2, "T1")
        logits(1, 0)
        row_max(0)
        value_time(1)
        exponent(0)
        scores(1, 1)
        q_out(2, False)
        v_piece(1, 256, 384, "gpsimd")
        v_piece(0, 0, 256, "scalar")
        q_quant(1)
        scores(2, 0)
        vs_spread(0)
        scores(2, 1)
        logits(1, 1)
        row_max(1)
        v_piece(1, 384, 512, "gpsimd")
        logits(2, 0)
        scores(3, 0)
        logits(2, 1)
        scores(3, 1)
        recip(0)
        q_quant(2)
        vs_spread(1)
        scores(4, 0)
        logits(3, 0)
        v_piece(0, 256, 512, "scalar")
        logits(3, 1)
        exponent(1)
        v_piece(1, 128, 256, "scalar")
        weigh(0)
        row_max(2)
        scores(4, 1)

        q_copy_at = {2: (3, 4), 3: (5, 6), 4: (7,)}
        q_quant_at = {3: 3, 4: 4, 5: 5, 6: 6, 7: 7}
        for i in range(2, 14):
            if i in q_quant_at:
                q_quant(q_quant_at[i])
            if i in (2, 3):
                v_quant(i - 2)
            if i >= 4:
                pg_quant(i - 4)
            if i >= 2:
                turn(i - 2)
            if i >= 4:
                values(i - 4, "U%d" % (i % 2))
            if i >= 3:
                interleave(i - 3, 0)
            if i >= 5:
                root_gap(i - 5)
            if i >= 3:
                interleave(i - 3, 1)
            if i >= 5:
                root_pow(i - 5)
            if i >= 9:
                res_piece(0, GSHARE * (i - 9), min(E, GSHARE * (i - 8)), "gpsimd")
            row_max(i + 1)
            if i >= 1:
                recip(i - 1)
            logits(i + 2, 0)
            logits(i + 2, 1)
            if i >= 1:
                weigh(i - 1)
            if i >= 2:
                gain_rows(i - 2)
                time_square(i - 2)
            exponent(i)
            for n, j in enumerate(q_copy_at.get(i, ())):
                q_turn(j, "T%d" % n)
                q_out(j, False)
            if i >= 5:
                finish(i - 5, False)
            if i >= 4:
                square_sum(i - 4)
            if i + 3 < TILES:
                scores(i + 3, 0)
                scores(i + 3, 1)

        interleave(11, 0)
        exponent(14)
        turn(12)
        pg_quant(10)
        root_gap_scalar(9)
        recip(13)
        row_max(15)
        values(10, "U0")
        gain_rows(12)
        weigh(13)
        interleave(11, 1)
        turn(13, ("S0", "S1"))
        root_pow(9)
        res_piece(0, 320, 416, "gpsimd")
        recip(14)
        exponent(15)
        pg_quant(11)
        weigh(14)
        gain_direct(13, 0)
        turn(14)
        finish(9, False)
        square_sum(10)
        recip(15)
        time_square(12)
        time_square(14)
        values(11, "U1")
        gain_direct(13, 1)
        interleave(12, 0)
        weigh(15)
        interleave(12, 1)
        pg_quant(13)
        root_gap_scalar(10)
        root_pow(10)
        pg_quant(12)
        square_sum(11)
        gain_direct(14, 0)
        turn(15, ("S0", "S1"))
        finish(10, False)
        root_gap(11)
        root_pow(11)
        values(12, "U0")
        gain_direct(14, 1)
        gain_direct(15, 0)
        res_piece(1, 0, 128, "scalar")
        res_piece(0, 416, 512, "scalar")
        square_sum(12)
        res_piece(1, 128, 256, "vector")
        pg_quant(14)
        finish(11, False)
        values(13, "V0")
        values(14, "V1")
        gain_direct(15, 1)
        time_square(13)
        root_gap_scalar(12)
        square_sum(13)
        root_pow(12)
        pg_quant(15)
        values(15, "T0")
        square_sum(14)
        res_piece(2, 0, 128, "vector")
        root_gap_scalar(13)
        time_square(15)
        root_pow(13)
        res_piece(1, 256, 384, "scalar")
        root_gap_scalar(14)
        res_piece(1, 384, 512, "vector")
        finish(12, True)
        res_quant(0)
        finish(13, True)
        square_sum(15)
        res_piece(2, 256, 384, "scalar")
        root_pow(14)
        res_piece(2, 128, 256, "vector")
        root_gap_scalar(15)
        res_piece(2, 384, 512, "scalar")
        finish(14, True)
        res_quant(1)
        root_pow(15)
        finish(15, False)
        res_quant(2)
        res_piece(3, 384, 512, "scalar")
        res_piece(3, 0, 384, "vector")
        res_quant(3)
